import numpy as np
import ml_dtypes


def mxq(x, axis, fmt="e4m3"):
    dtype, down = {"e4m3": (ml_dtypes.float8_e4m3fn, 7), "e5m2": (ml_dtypes.float8_e5m2, 14)}[fmt]
    v = np.moveaxis(np.asarray(x, np.float32).astype(ml_dtypes.bfloat16).astype(np.float64), axis, -1)
    blocks = v.reshape(v.shape[:-1] + (-1, 32))
    amax = np.abs(blocks).max(-1, keepdims=True)
    byte = np.maximum(np.where(amax > 0, np.frexp(amax)[1] - 1 + 127, 0) - down, 1)
    scale = np.exp2(byte - 127.0)
    codes = (blocks / scale).astype(np.float32).astype(dtype).astype(np.float64)
    return np.moveaxis((codes * scale).reshape(v.shape), -1, axis)


WIDE = False


def mx_kscale(k, group=512):
    if not WIDE:
        return np.ones(k)
    levels = np.array([10, -10, 5, -5, 0])
    if group != 512:
        return np.exp2(np.random.permutation(np.resize(levels, k // group))).repeat(group)
    if k % 512:
        return np.exp2(np.random.permutation(np.resize(levels, k // 32))).repeat(32)
    a = np.empty((k // 512, 16))
    for p in range(k // 512):
        a[p, :8] = np.random.permutation(np.resize(levels, 8))
        for g in range(8):
            far = levels[np.abs(levels - a[p, g]) >= 10]
            a[p, g + 8] = far[np.random.randint(len(far))]
    return np.exp2(a.ravel()).repeat(32)


def f64(x):
    return np.asarray(x).astype(np.float64)


def striped(idx):
    return np.tile(np.asarray(idx).reshape(-1, 16).T, (8, 1)).astype(np.uint16)


def unstriped(offs):
    return offs[:16].T.reshape(-1).astype(np.int64)


H, KV, D, NQ, N = 4, 2, 256, 512, 512


def setup_inputs():
    n = np.random.standard_normal
    s = mx_kscale(D, 0)[:, None]
    u = mx_kscale(N)
    t = np.random.uniform(0.5, 2.0, N) * u
    v = n((KV, N, 128))
    return {
        "qT": (n((H, D, NQ)) * s * (0.70 / np.sqrt(D))).astype(np.float32),
        "kT": (n((KV, D, N)) / s).astype(np.float32),
        "t": t.reshape(N, 1).astype(np.float32),
        "v": (v / t[:, None]).astype(np.float32),
        "kb": (0.5 * n((N, 1))).astype(np.float32),
        "gn": np.tile(np.random.uniform(0.5, 2.0, 128), (128, 1)).astype(np.float32),
    }


def reference(qT, kT, t, v, kb, gn):
    a = np.repeat(mxq(f64(kT), 1, "e4m3"), H // KV, 0).transpose(0, 2, 1) @ mxq(f64(qT), 1, "e4m3")
    a = a + f64(kb)
    p = np.tanh(a)
    w = p * f64(t)
    y = mxq(w, 1, "e4m3").transpose(0, 2, 1) @ np.repeat(mxq(f64(v), 1, "e4m3"), H // KV, 0)
    y = y / 16.0
    y = y / np.sqrt(np.mean(np.square(y), -1, keepdims=True) + 1e-5) * f64(gn)[:1]
    return y

@@ -1,0 +1,321 @@
+from contextlib import ExitStack
+
+import concourse.mybir as mybir
+
+H, KV, D, NQ, N, E = 4, 2, 256, 512, 512, 128
+FLOPS = 2 * H * NQ * N * (D + E)
+
+F32 = mybir.dt.float32
+BF16 = mybir.dt.bfloat16
+U32 = mybir.dt.uint32
+U8 = mybir.dt.uint8
+FP8X4 = mybir.dt.float8_e4m3fn_x4
+ACT = mybir.ActivationFunctionType
+ALU = mybir.AluOpType
+
+P = 128
+PACK = 4
+ROWS = 64
+BANK = 512
+RUN = 2
+PAIRS = ((1, 2), (0, 3))
+UNITS = ((0, 0, 128), (0, 128, 128), (0, 256, 256), (1, 0, 256), (1, 256, 256))
+ORDER = (
+    ("load_small",),
+    ("load_k", 0, 512),
+    ("load_q", 0),
+    ("spread_k", "act", 0, 40),
+    ("load_q", 1),
+    ("spread_k", "dve", 40, 128),
+    ("load_q", 2),
+    ("spread_q", 0, "dve", 0, 128),
+    ("quant_k", 0, 1),
+    ("quant_q", 0),
+    ("load_q", 3, 0),
+    ("quant_k", 1, 2),
+    ("quant_k", 2, 3),
+    ("quant_k", 3, 4),
+    ("load_q", 4, 0),
+    ("spread_q", 1, "act", 0, 128),
+    ("scores", 0, (0, 1, 2, 3)),
+    ("load_v",),
+    ("quant_q", 1),
+    ("load_gn",),
+    ("load_q", 3, 1),
+    ("spread_q", 2, "dve", 0, 256),
+    ("load_q", 4, 1),
+    ("quant_q", 2),
+    ("tanh", 0, 0, (0, 1, 2, 3)),
+    ("tanh", 0, 1, (0, 1, 2, 3)),
+    ("scores", 1, (0, 1, 2, 3)),
+    ("weigh", 0, 0),
+    ("weigh", 0, 1),
+    ("tanh", 1, 0, (0, 1, 2, 3)),
+    ("tanh", 1, 1, (0, 1, 2, 3)),
+    ("spread_q", 3, "dve", 0, 256),
+    ("weigh", 1, 0),
+    ("scores", 2, (0, 1)),
+    ("quant_q", 3),
+    ("tanh", 2, 1, (0, 1)),
+    ("scores", 2, (2, 3)),
+    ("quant_w", 1, 0),
+    ("quant_w", 0, 1),
+    ("tanh", 2, 0, (0, 1)),
+    ("tanh", 2, 0, (2, 3)),
+    ("spread_q", 4, "dve", 0, 256),
+    ("spread_v", 1, "dve"),
+    ("quant_q", 4),
+    ("tanh", 2, 1, (2, 3)),
+    ("scores", 3, (0, 1)),
+    ("scores", 3, (2, 3)),
+    ("quant_w", 0, 0),
+    ("weigh", 2, 0),
+    ("spread_v", 0, "act"),
+    ("quant_v",),
+    ("quant_w", 2, 0),
+    ("values", 0, 0),
+    ("tanh", 3, 0, (0, 1)),
+    ("tanh", 3, 1, (0, 1)),
+    ("scores", 4, (0, 1)),
+    ("weigh", 2, 1),
+    ("tanh", 3, 0, (2, 3)),
+    ("values", 2, 0),
+    ("sum_squares", 0, 0),
+    ("weigh", 3, 0),
+    ("weigh", 1, 1),
+    ("quant_w", 2, 1),
+    ("tanh", 3, 1, (2, 3)),
+    ("values", 0, 1),
+    ("tanh", 4, 0, (0, 1)),
+    ("scores", 4, (2, 3)),
+    ("sum_squares", 0, 1),
+    ("values", 1, 0),
+    ("tanh", 4, 1, (0, 1)),
+    ("sum_squares", 2, 0),
+    ("quant_w", 1, 1),
+    ("tanh", 4, 0, (2, 3)),
+    ("quant_w", 3, 0),
+    ("values", 2, 1),
+    ("sum_squares", 1, 0),
+    ("tanh", 4, 1, (2, 3)),
+    ("weigh", 3, 1),
+    ("weigh", 4, 0),
+    ("quant_w", 3, 1),
+    ("values", 1, 1),
+    ("quant_w", 4, 0),
+    ("sum_squares", 2, 1),
+    ("weigh", 4, 1),
+    ("sum_squares", 1, 1),
+    ("roots", 0, 8),
+    ("finish", 0, 0),
+    ("values", 3, 0),
+    ("sum_squares", 3, 0),
+    ("values", 4, 0),
+    ("finish", 0, 1),
+    ("quant_w", 4, 1),
+    ("sum_squares", 4, 0),
+    ("values", 3, 1),
+    ("values", 4, 1),
+    ("finish", 1, 1),
+    ("sum_squares", 3, 1),
+    ("roots", 8, 12),
+    ("finish", 1, 0),
+    ("finish", 2, 1),
+    ("sum_squares", 4, 1),
+    ("finish", 2, 0),
+    ("roots", 12, 16),
+    ("warm_sqrt",),
+    ("finish", 3, 0),
+    ("finish", 3, 1),
+    ("finish", 4, 0),
+    ("finish", 4, 1),
+)
+
+
+def tile_rows_a_tanh_kb_onorm_kernel(tc, qT, kT, t, v, kb, gn, out):
+    nc = tc.nc
+    with ExitStack() as ctx:
+        sb = ctx.enter_context(tc.tile_pool(name="sb", bufs=1))
+        ps = ctx.enter_context(tc.psum_pool(name="ps", bufs=1))
+        ctx.enter_context(tc.manual_schedule())
+
+        def sbuf(name, shape, dtype):
+            return sb.tile(shape, dtype, name=name, align_bytes=64)
+
+        def mx_pair(name, cols):
+            return sbuf(name + "_codes", [P, cols], U32), sbuf(name + "_scales", [P, cols], U8)
+
+        score = [[ps.tile([P, BANK], F32, name="score%d%d" % (g, b)) for b in range(2)] for g in range(2)]
+        ybank = [ps.tile([P, BANK], F32, name="y%d" % b) for b in range(4)]
+
+        nu = len(UNITS)
+        width = [u[2] for u in UNITS]
+        first = [sum(2 * w // P for w in width[:u]) for u in range(nu)]
+
+        k_raw = sbuf("k_raw", [P, PACK, N], F32)
+        k_bf = sbuf("k_bf", [P, N * PACK], BF16)
+        k_mx = mx_pair("k", N)
+        v_raw = sbuf("v_raw", [P, KV, PACK, E], F32)
+        v_bf = sbuf("v_bf", [P, KV * E * PACK], BF16)
+        v_mx = mx_pair("v", KV * E)
+        t_sb = sbuf("t_sb", [P, PACK], F32)
+        kb_sb = sbuf("kb_sb", [P, PACK], F32)
+        gn_sb = sbuf("gn_sb", [P, E], F32)
+        q_raw = [sbuf("q_raw%d" % u, [P, PACK, width[u]], F32) for u in range(nu)]
+        q_bf = [sbuf("q_bf%d" % u, [P, width[u] * PACK], BF16) for u in range(nu)]
+        q_mx = [mx_pair("q%d" % u, width[u]) for u in range(nu)]
+        p_sb = [[sbuf("p%d%d" % (u, g), [P, PACK, width[u]], F32) for g in range(2)] for u in range(nu)]
+        w_bf = [[sbuf("w%d%d" % (u, g), [P, width[u] * PACK], BF16) for g in range(2)] for u in range(nu)]
+        w_mx = [[mx_pair("w%d%d" % (u, g), width[u]) for g in range(2)] for u in range(nu)]
+        o_sb = [[sbuf("o%d%d" % (u, g), [P, width[u]], F32) for g in range(2)] for u in range(nu)]
+        squares = sbuf("squares", [P, 16 * E], BF16)
+        ssq = sbuf("ssq", [P, 16], F32)
+        rstd = sbuf("rstd", [P, 16], F32)
+        warm = sbuf("warm", [P, 8], F32)
+
+        q_rows = qT.rearrange("h d n -> (h d) n")
+        k_rows = kT.rearrange("h (p j) n -> (h p) j n", j=PACK)
+
+        def copy(engine, dst, src):
+            if engine == "act":
+                nc.scalar.copy(out=dst, in_=src)
+            else:
+                nc.vector.tensor_copy(out=dst, in_=src)
+
+        def load_q(u, g=None):
+            pair, q0, w = UNITS[u]
+            queue = nc.scalar if g == 1 else nc.sync
+            if g is None:
+                rows = q_rows[PAIRS[pair][0] * D : (PAIRS[pair][1] + 1) * D, q0 : q0 + w]
+                queue.dma_start(out=q_raw[u][:], in_=rows.rearrange("(p j) n -> p j n", j=PACK))
+            else:
+                rows = q_rows[PAIRS[pair][g] * D : (PAIRS[pair][g] + 1) * D, q0 : q0 + w]
+                queue.dma_start(out=q_raw[u][g * ROWS : (g + 1) * ROWS], in_=rows.rearrange("(p j) n -> p j n", j=PACK))
+
+        def load_k(lo, hi):
+            nc.sync.dma_start(out=k_raw[:, :, lo:hi], in_=k_rows[:, :, lo:hi])
+
+        def spread_k(engine, lo, hi):
+            dst = k_bf[:].rearrange("p (r s j) -> p s j r", r=PACK, j=PACK)[:, lo:hi]
+            src = k_raw[:].rearrange("p j (s r) -> p s j r", r=PACK)[:, lo:hi]
+            copy(engine, dst, src)
+
+        def spread_q(u, engine, lo=0, hi=None):
+            hi = hi or width[u]
+            dst = q_bf[u][:].rearrange("p (c i j) -> p c j i", i=RUN, j=PACK)[:, lo // RUN : hi // RUN]
+            src = q_raw[u][:].rearrange("p j (c i) -> p c j i", i=RUN)[:, lo // RUN : hi // RUN]
+            copy(engine, dst, src)
+
+        def spread_v(kv, engine):
+            dst = v_bf[:, kv * E * PACK : (kv + 1) * E * PACK].rearrange("p (c i j) -> p c j i", i=RUN, j=PACK)
+            src = v_raw[:, kv].rearrange("p j (c i) -> p c j i", i=RUN)
+            copy(engine, dst, src)
+
+        def quantize(mx, bf, lo, hi):
+            nc.vector.quantize_mx(out=mx[0][:, lo:hi].bitcast(FP8X4), scales=mx[1][:, lo:hi], in_=bf[:, lo * PACK : hi * PACK])
+
+        def matmul(dst, a, a_at, b, b_at, rows):
+            nc.tensor.matmul_mx(
+                out=dst,
+                lhsT=a[0][rows, a_at : a_at + P].bitcast(FP8X4),
+                lhsT_scale=a[1][rows, a_at : a_at + P],
+                rhs=b[0][rows, b_at : b_at + P].bitcast(FP8X4),
+                rhs_scale=b[1][rows, b_at : b_at + P],
+                start=True,
+                stop=True,
+            )
+
+        def place(u, g, r):
+            per_bank = BANK // width[u]
+            base = sum(PACK * w // BANK for w in width[:u])
+            return score[g][(base + r // per_bank) % 2], (r % per_bank) * width[u]
+
+        def scores(u, rs):
+            for r in rs:
+                for c in range(0, width[u], P):
+                    for g in range(2):
+                        bank, at = place(u, g, r)
+                        matmul(bank[:, at + c : at + c + P], k_mx, r * P, q_mx[u], c, slice(g * ROWS, (g + 1) * ROWS))
+
+        def tanh(u, g, rs):
+            for r in rs:
+                bank, at = place(u, g, r)
+                n = width[u] // P
+                nc.scalar.activation(
+                    out=p_sb[u][g][:, r, :].rearrange("p (i m) -> p i m", i=n),
+                    in_=bank[:, at : at + width[u]].rearrange("p (m i) -> p i m", i=n),
+                    func=ACT.Tanh,
+                    bias=kb_sb[:, r : r + 1],
+                )
+
+        def weigh(u, g):
+            nc.vector.tensor_tensor(
+                out=w_bf[u][g][:].rearrange("p (c i r) -> p c r i", i=RUN, r=PACK),
+                in0=p_sb[u][g][:].rearrange("p r (c i) -> p c r i", i=RUN),
+                in1=t_sb[:].unsqueeze(1).unsqueeze(3).to_broadcast([P, width[u] // RUN, PACK, RUN]),
+                op=ALU.mult,
+            )
+
+        def quant_w(u, g):
+            quantize(w_mx[u][g], w_bf[u][g], 0, width[u])
+
+        def tiles(u, g):
+            n = width[u] // P
+            return range(first[u] + g * n, first[u] + (g + 1) * n)
+
+        def y_of(i):
+            return ybank[i // 4][:, (i % 4) * E : (i % 4 + 1) * E]
+
+        def values(u, g):
+            for n, i in enumerate(tiles(u, g)):
+                matmul(y_of(i), w_mx[u][g], n * P, v_mx, g * E, slice(0, P))
+
+        def sum_squares(u, g):
+            for i in tiles(u, g):
+                nc.scalar.activation(out=squares[:, i * E : (i + 1) * E], in_=y_of(i), func=ACT.Square, accum_out=ssq[:, i : i + 1])
+
+        def roots(lo, hi):
+            nc.scalar.activation(out=rstd[:, lo:hi], in_=ssq[:, lo:hi], func=ACT.Abs_reciprocal_sqrt, scale=1.0 / E, bias=256 * 1e-5)
+
+        def finish(u, g):
+            pair, q0, w = UNITS[u]
+            for n, i in enumerate(tiles(u, g)):
+                nc.vector.scalar_tensor_tensor(
+                    out=o_sb[u][g][:, n * E : (n + 1) * E], in0=y_of(i), scalar=rstd[:, i : i + 1], in1=gn_sb[:], op0=ALU.mult, op1=ALU.mult
+                )
+            rows = out[PAIRS[pair][g], q0 : q0 + w, :].rearrange("(m i) e -> m (i e)", m=P)
+            nc.sync.dma_start(out=rows, in_=o_sb[u][g][:])
+
+        def load_small():
+            nc.scalar.dma_start(out=kb_sb[:], in_=kb.rearrange("(p j) o -> p (j o)", j=PACK))
+            nc.scalar.dma_start(out=t_sb[:], in_=t.rearrange("(p j) o -> p (j o)", j=PACK))
+            nc.vector.memset(warm[:, 0:1], 1.0)
+            nc.scalar.activation(out=warm[:, 1:2], in_=warm[:, 0:1], func=ACT.Tanh)
+
+        def load_v():
+            nc.sync.dma_start(out=v_raw[:], in_=v.rearrange("h (p j) e -> p h j e", j=PACK))
+
+        def load_gn():
+            nc.sync.dma_start(out=gn_sb[:], in_=gn)
+
+        def warm_sqrt():
+            nc.scalar.activation(out=warm[:, 2:3], in_=warm[:, 0:1], func=ACT.Abs_reciprocal_sqrt)
+
+        def quant_k(lo, hi):
+            quantize(k_mx, k_bf, lo * P, hi * P)
+
+        def quant_q(u):
+            quantize(q_mx[u], q_bf[u], 0, width[u])
+
+        def quant_v():
+            quantize(v_mx, v_bf, 0, KV * E)
+
+        steps = {
+            "load_small": load_small, "load_k": load_k, "load_q": load_q, "load_v": load_v, "load_gn": load_gn,
+            "spread_k": spread_k, "spread_q": spread_q, "spread_v": spread_v,
+            "quant_k": quant_k, "quant_q": quant_q, "quant_v": quant_v, "quant_w": quant_w,
+            "scores": scores, "tanh": tanh, "weigh": weigh, "values": values, "warm_sqrt": warm_sqrt,
+            "sum_squares": sum_squares, "roots": roots, "finish": finish,
+        }
+        for step in ORDER:
+            steps[step[0]](*step[1:])

@@ -17,116 +17,118 @@ P = 128
 PACK = 4
 ROWS = 64
 BANK = 512
-RUN = 2
+RUN = 4
 PAIRS = ((1, 2), (0, 3))
 UNITS = ((0, 0, 128), (0, 128, 128), (0, 256, 256), (1, 0, 256), (1, 256, 256))
 ORDER = (
     ("load_small",),
     ("load_k", 0, 512),
     ("load_q", 0),
-    ("spread_k", "act", 0, 40),
     ("load_q", 1),
-    ("spread_k", "dve", 40, 128),
     ("load_q", 2),
+    ("load_q", 3, 0),
+    ("load_q", 4, 0),
+    ("load_v",),
+    ("load_gn",),
+    ("spread_k", "act", 0, 40),
+    ("spread_k", "dve", 40, 128),
+    ("load_q", 3, 1),
+    ("load_q", 4, 1),
     ("spread_q", 0, "dve", 0, 128),
     ("quant_k", 0, 1),
     ("quant_q", 0),
-    ("load_q", 3, 0),
     ("quant_k", 1, 2),
+    ("spread_q", 1, "act", 0, 128),
     ("quant_k", 2, 3),
     ("quant_k", 3, 4),
-    ("load_q", 4, 0),
-    ("spread_q", 1, "act", 0, 128),
     ("scores", 0, (0, 1, 2, 3)),
-    ("load_v",),
     ("quant_q", 1),
-    ("load_gn",),
-    ("load_q", 3, 1),
-    ("spread_q", 2, "dve", 0, 256),
-    ("load_q", 4, 1),
-    ("quant_q", 2),
     ("tanh", 0, 0, (0, 1, 2, 3)),
-    ("tanh", 0, 1, (0, 1, 2, 3)),
     ("scores", 1, (0, 1, 2, 3)),
+    ("spread_q", 2, "dve", 0, 256),
+    ("tanh", 0, 1, (0, 1, 2, 3)),
+    ("quant_q", 2),
     ("weigh", 0, 0),
-    ("weigh", 0, 1),
     ("tanh", 1, 0, (0, 1, 2, 3)),
-    ("tanh", 1, 1, (0, 1, 2, 3)),
-    ("spread_q", 3, "dve", 0, 256),
-    ("weigh", 1, 0),
     ("scores", 2, (0, 1)),
-    ("quant_q", 3),
-    ("tanh", 2, 1, (0, 1)),
-    ("scores", 2, (2, 3)),
-    ("quant_w", 1, 0),
-    ("quant_w", 0, 1),
-    ("tanh", 2, 0, (0, 1)),
-    ("tanh", 2, 0, (2, 3)),
-    ("spread_q", 4, "dve", 0, 256),
-    ("spread_v", 1, "dve"),
-    ("quant_q", 4),
-    ("tanh", 2, 1, (2, 3)),
-    ("scores", 3, (0, 1)),
-    ("scores", 3, (2, 3)),
+    ("weigh", 0, 1),
+    ("tanh", 1, 1, (0, 1, 2, 3)),
     ("quant_w", 0, 0),
+    ("scores", 2, (2, 3)),
+    ("spread_q", 3, "dve", 0, 256),
+    ("tanh", 2, 0, (0, 1)),
+    ("weigh", 1, 0),
+    ("tanh", 2, 1, (0, 1)),
+    ("quant_q", 3),
+    ("quant_w", 0, 1),
+    ("tanh", 2, 0, (2, 3)),
+    ("weigh", 1, 1),
+    ("scores", 3, (0, 1)),
+    ("tanh", 2, 1, (2, 3)),
+    ("spread_q", 4, "dve", 0, 256),
+    ("scores", 3, (2, 3)),
     ("weigh", 2, 0),
-    ("spread_v", 0, "act"),
-    ("quant_v",),
-    ("quant_w", 2, 0),
-    ("values", 0, 0),
     ("tanh", 3, 0, (0, 1)),
+    ("spread_v", 0, "act"),
+    ("spread_v", 1, "dve"),
     ("tanh", 3, 1, (0, 1)),
+    ("quant_q", 4),
+    ("quant_v",),
+    ("tanh", 3, 1, (2, 3)),
     ("scores", 4, (0, 1)),
+    ("quant_w", 2, 0),
+    ("quant_w", 1, 1),
     ("weigh", 2, 1),
     ("tanh", 3, 0, (2, 3)),
     ("values", 2, 0),
-    ("sum_squares", 0, 0),
-    ("weigh", 3, 0),
-    ("weigh", 1, 1),
-    ("quant_w", 2, 1),
-    ("tanh", 3, 1, (2, 3)),
-    ("values", 0, 1),
+    ("values", 0, 0),
     ("tanh", 4, 0, (0, 1)),
     ("scores", 4, (2, 3)),
-    ("sum_squares", 0, 1),
-    ("values", 1, 0),
-    ("tanh", 4, 1, (0, 1)),
+    ("weigh", 3, 0),
+    ("sum_squares", 0, 0),
     ("sum_squares", 2, 0),
-    ("quant_w", 1, 1),
+    ("values", 0, 1),
     ("tanh", 4, 0, (2, 3)),
-    ("quant_w", 3, 0),
-    ("values", 2, 1),
-    ("sum_squares", 1, 0),
-    ("tanh", 4, 1, (2, 3)),
+    ("quant_w", 2, 1),
+    ("quant_w", 1, 0),
+    ("sum_squares", 0, 1),
     ("weigh", 3, 1),
+    ("tanh", 4, 1, (0, 1)),
+    ("values", 1, 0),
+    ("values", 2, 1),
+    ("tanh", 4, 1, (2, 3)),
     ("weigh", 4, 0),
-    ("quant_w", 3, 1),
+    ("sum_squares", 1, 0),
     ("values", 1, 1),
-    ("quant_w", 4, 0),
-    ("sum_squares", 2, 1),
-    ("weigh", 4, 1),
-    ("sum_squares", 1, 1),
-    ("roots", 0, 8),
-    ("finish", 0, 0),
+    ("quant_w", 3, 0),
+    ("quant_w", 3, 1),
     ("values", 3, 0),
+    ("quant_w", 4, 0),
+    ("weigh", 4, 1),
+    ("roots", 0, 2),
+    ("sum_squares", 1, 1),
     ("sum_squares", 3, 0),
     ("values", 4, 0),
-    ("finish", 0, 1),
-    ("quant_w", 4, 1),
-    ("sum_squares", 4, 0),
+    ("roots", 2, 4),
+    ("sum_squares", 2, 1),
     ("values", 3, 1),
-    ("values", 4, 1),
+    ("finish", 0, 1),
+    ("sum_squares", 4, 0),
+    ("finish", 0, 0),
     ("finish", 1, 1),
+    ("roots", 4, 8),
     ("sum_squares", 3, 1),
-    ("roots", 8, 12),
+    ("quant_w", 4, 1),
     ("finish", 1, 0),
+    ("finish", 2, 0),
+    ("roots", 8, 12),
+    ("values", 4, 1),
     ("finish", 2, 1),
     ("sum_squares", 4, 1),
-    ("finish", 2, 0),
-    ("roots", 12, 16),
-    ("warm_sqrt",),
     ("finish", 3, 0),
     ("finish", 3, 1),
+    ("roots", 12, 14),
+    ("roots", 14, 16),
     ("finish", 4, 0),
     ("finish", 4, 1),
 )
@@ -200,10 +202,11 @@ def tile_rows_a_tanh_kb_onorm_kernel(tc, qT, kT, t, v, kb, gn, out):
             src = k_raw[:].rearrange("p j (s r) -> p s j r", r=PACK)[:, lo:hi]
             copy(engine, dst, src)
 
-        def spread_q(u, engine, lo=0, hi=None):
-            hi = hi or width[u]
-            dst = q_bf[u][:].rearrange("p (c i j) -> p c j i", i=RUN, j=PACK)[:, lo // RUN : hi // RUN]
-            src = q_raw[u][:].rearrange("p j (c i) -> p c j i", i=RUN)[:, lo // RUN : hi // RUN]
+        def spread_q(u, engine, lo, hi):
+            n = width[u] // P
+            run = RUN if engine == "dve" or n == 1 else n
+            dst = q_bf[u][:].rearrange("p (i c m j) -> p c j m i", i=n, m=run // n, j=PACK)[:, lo // run : hi // run]
+            src = q_raw[u][:].rearrange("p j (c m i) -> p c j m i", i=n, m=run // n)[:, lo // run : hi // run]
             copy(engine, dst, src)
 
         def spread_v(kv, engine):
@@ -240,10 +243,9 @@ def tile_rows_a_tanh_kb_onorm_kernel(tc, qT, kT, t, v, kb, gn, out):
         def tanh(u, g, rs):
             for r in rs:
                 bank, at = place(u, g, r)
-                n = width[u] // P
                 nc.scalar.activation(
-                    out=p_sb[u][g][:, r, :].rearrange("p (i m) -> p i m", i=n),
-                    in_=bank[:, at : at + width[u]].rearrange("p (m i) -> p i m", i=n),
+                    out=p_sb[u][g][:, r, :],
+                    in_=bank[:, at : at + width[u]],
                     func=ACT.Tanh,
                     bias=kb_sb[:, r : r + 1],
                 )
@@ -298,9 +300,6 @@ def tile_rows_a_tanh_kb_onorm_kernel(tc, qT, kT, t, v, kb, gn, out):
         def load_gn():
             nc.sync.dma_start(out=gn_sb[:], in_=gn)
 
-        def warm_sqrt():
-            nc.scalar.activation(out=warm[:, 2:3], in_=warm[:, 0:1], func=ACT.Abs_reciprocal_sqrt)
-
         def quant_k(lo, hi):
             quantize(k_mx, k_bf, lo * P, hi * P)
 
@@ -314,7 +313,7 @@ def tile_rows_a_tanh_kb_onorm_kernel(tc, qT, kT, t, v, kb, gn, out):
             "load_small": load_small, "load_k": load_k, "load_q": load_q, "load_v": load_v, "load_gn": load_gn,
             "spread_k": spread_k, "spread_q": spread_q, "spread_v": spread_v,
             "quant_k": quant_k, "quant_q": quant_q, "quant_v": quant_v, "quant_w": quant_w,
-            "scores": scores, "tanh": tanh, "weigh": weigh, "values": values, "warm_sqrt": warm_sqrt,
+            "scores": scores, "tanh": tanh, "weigh": weigh, "values": values,
             "sum_squares": sum_squares, "roots": roots, "finish": finish,
         }
         for step in ORDER:

@@ -18,11 +18,13 @@ PACK = 4
 ROWS = 64
 BANK = 512
 RUN = 4
+WRUN = 8
 PAIRS = ((1, 2), (0, 3))
 UNITS = ((0, 0, 128), (0, 128, 128), (0, 256, 256), (1, 0, 256), (1, 256, 256))
 ORDER = (
     ("load_small",),
     ("load_k", 0, 512),
+    ("spread_t",),
     ("load_q", 0),
     ("load_q", 1),
     ("load_q", 2),
@@ -161,6 +163,7 @@ def tile_rows_a_tanh_kb_onorm_kernel(tc, qT, kT, t, v, kb, gn, out):
         v_bf = sbuf("v_bf", [P, KV * E * PACK], BF16)
         v_mx = mx_pair("v", KV * E)
         t_sb = sbuf("t_sb", [P, PACK], F32)
+        t_run = sbuf("t_run", [P, PACK, WRUN], F32)
         kb_sb = sbuf("kb_sb", [P, PACK], F32)
         gn_sb = sbuf("gn_sb", [P, E], F32)
         q_raw = [sbuf("q_raw%d" % u, [P, PACK, width[u]], F32) for u in range(nu)]
@@ -252,9 +255,9 @@ def tile_rows_a_tanh_kb_onorm_kernel(tc, qT, kT, t, v, kb, gn, out):
 
         def weigh(u, g):
             nc.vector.tensor_tensor(
-                out=w_bf[u][g][:].rearrange("p (c i r) -> p c r i", i=RUN, r=PACK),
-                in0=p_sb[u][g][:].rearrange("p r (c i) -> p c r i", i=RUN),
-                in1=t_sb[:].unsqueeze(1).unsqueeze(3).to_broadcast([P, width[u] // RUN, PACK, RUN]),
+                out=w_bf[u][g][:].rearrange("p (c i r) -> p c r i", i=WRUN, r=PACK),
+                in0=p_sb[u][g][:].rearrange("p r (c i) -> p c r i", i=WRUN),
+                in1=t_run[:].unsqueeze(1).to_broadcast([P, width[u] // WRUN, PACK, WRUN]),
                 op=ALU.mult,
             )
 
@@ -294,6 +297,9 @@ def tile_rows_a_tanh_kb_onorm_kernel(tc, qT, kT, t, v, kb, gn, out):
             nc.vector.memset(warm[:, 0:1], 1.0)
             nc.scalar.activation(out=warm[:, 1:2], in_=warm[:, 0:1], func=ACT.Tanh)
 
+        def spread_t():
+            nc.vector.tensor_copy(out=t_run[:], in_=t_sb[:].unsqueeze(2).to_broadcast([P, PACK, WRUN]))
+
         def load_v():
             nc.sync.dma_start(out=v_raw[:], in_=v.rearrange("h (p j) e -> p h j e", j=PACK))
 
@@ -310,7 +316,7 @@ def tile_rows_a_tanh_kb_onorm_kernel(tc, qT, kT, t, v, kb, gn, out):
             quantize(v_mx, v_bf, 0, KV * E)
 
         steps = {
-            "load_small": load_small, "load_k": load_k, "load_q": load_q, "load_v": load_v, "load_gn": load_gn,
+            "load_small": load_small, "load_k": load_k, "load_q": load_q, "load_v": load_v, "load_gn": load_gn, "spread_t": spread_t,
             "spread_k": spread_k, "spread_q": spread_q, "spread_v": spread_v,
             "quant_k": quant_k, "quant_q": quant_q, "quant_v": quant_v, "quant_w": quant_w,
             "scores": scores, "tanh": tanh, "weigh": weigh, "values": values,

from contextlib import ExitStack

import concourse.mybir as mybir

H, KV, D, NQ, N, E = 4, 2, 256, 512, 512, 128
FLOPS = 2 * H * NQ * N * (D + E)

F32 = mybir.dt.float32
BF16 = mybir.dt.bfloat16
U32 = mybir.dt.uint32
U8 = mybir.dt.uint8
FP8X4 = mybir.dt.float8_e4m3fn_x4
ACT = mybir.ActivationFunctionType
ALU = mybir.AluOpType

P = 128
PACK = 4
ROWS = 64
BANK = 512
RUN = 4
WRUN = 8
PAIRS = ((1, 2), (0, 3))
UNITS = ((0, 0, 128), (0, 128, 128), (0, 256, 256), (1, 0, 256), (1, 256, 256))
ORDER = (
    ("load_small",),
    ("load_k", 0, 512),
    ("spread_t",),
    ("load_q", 0),
    ("load_q", 1),
    ("load_q", 2),
    ("load_q", 3, 0),
    ("load_q", 4, 0),
    ("load_v",),
    ("load_gn",),
    ("spread_k", "act", 0, 40),
    ("spread_k", "dve", 40, 128),
    ("load_q", 3, 1),
    ("load_q", 4, 1),
    ("spread_q", 0, "dve", 0, 128),
    ("quant_k", 0, 1),
    ("quant_q", 0),
    ("quant_k", 1, 2),
    ("spread_q", 1, "act", 0, 128),
    ("quant_k", 2, 3),
    ("quant_k", 3, 4),
    ("scores", 0, (0, 1, 2, 3)),
    ("quant_q", 1),
    ("tanh", 0, 0, (0, 1, 2, 3)),
    ("scores", 1, (0, 1, 2, 3)),
    ("spread_q", 2, "dve", 0, 256),
    ("tanh", 0, 1, (0, 1, 2, 3)),
    ("quant_q", 2),
    ("weigh", 0, 0),
    ("tanh", 1, 0, (0, 1, 2, 3)),
    ("scores", 2, (0, 1)),
    ("weigh", 0, 1),
    ("tanh", 1, 1, (0, 1, 2, 3)),
    ("quant_w", 0, 0),
    ("scores", 2, (2, 3)),
    ("spread_q", 3, "dve", 0, 256),
    ("tanh", 2, 0, (0, 1)),
    ("weigh", 1, 0),
    ("tanh", 2, 1, (0, 1)),
    ("quant_q", 3),
    ("quant_w", 0, 1),
    ("tanh", 2, 0, (2, 3)),
    ("weigh", 1, 1),
    ("scores", 3, (0, 1)),
    ("tanh", 2, 1, (2, 3)),
    ("spread_q", 4, "dve", 0, 256),
    ("scores", 3, (2, 3)),
    ("weigh", 2, 0),
    ("tanh", 3, 0, (0, 1)),
    ("spread_v", 0, "act"),
    ("spread_v", 1, "dve"),
    ("tanh", 3, 1, (0, 1)),
    ("quant_q", 4),
    ("quant_v",),
    ("tanh", 3, 1, (2, 3)),
    ("scores", 4, (0, 1)),
    ("quant_w", 2, 0),
    ("quant_w", 1, 1),
    ("weigh", 2, 1),
    ("tanh", 3, 0, (2, 3)),
    ("values", 2, 0),
    ("values", 0, 0),
    ("tanh", 4, 0, (0, 1)),
    ("scores", 4, (2, 3)),
    ("weigh", 3, 0),
    ("sum_squares", 0, 0),
    ("sum_squares", 2, 0),
    ("values", 0, 1),
    ("tanh", 4, 0, (2, 3)),
    ("quant_w", 2, 1),
    ("quant_w", 1, 0),
    ("sum_squares", 0, 1),
    ("weigh", 3, 1),
    ("tanh", 4, 1, (0, 1)),
    ("values", 1, 0),
    ("values", 2, 1),
    ("tanh", 4, 1, (2, 3)),
    ("weigh", 4, 0),
    ("sum_squares", 1, 0),
    ("values", 1, 1),
    ("quant_w", 3, 0),
    ("quant_w", 3, 1),
    ("values", 3, 0),
    ("quant_w", 4, 0),
    ("weigh", 4, 1),
    ("roots", 0, 2),
    ("sum_squares", 1, 1),
    ("sum_squares", 3, 0),
    ("values", 4, 0),
    ("roots", 2, 4),
    ("sum_squares", 2, 1),
    ("values", 3, 1),
    ("finish", 0, 1),
    ("sum_squares", 4, 0),
    ("finish", 0, 0),
    ("finish", 1, 1),
    ("roots", 4, 8),
    ("sum_squares", 3, 1),
    ("quant_w", 4, 1),
    ("finish", 1, 0),
    ("finish", 2, 0),
    ("roots", 8, 12),
    ("values", 4, 1),
    ("finish", 2, 1),
    ("sum_squares", 4, 1),
    ("finish", 3, 0),
    ("finish", 3, 1),
    ("roots", 12, 14),
    ("roots", 14, 16),
    ("finish", 4, 0),
    ("finish", 4, 1),
)


def tile_rows_a_tanh_kb_onorm_kernel(tc, qT, kT, t, v, kb, gn, out):
    nc = tc.nc
    with ExitStack() as ctx:
        sb = ctx.enter_context(tc.tile_pool(name="sb", bufs=1))
        ps = ctx.enter_context(tc.psum_pool(name="ps", bufs=1))
        ctx.enter_context(tc.manual_schedule())

        def sbuf(name, shape, dtype):
            return sb.tile(shape, dtype, name=name, align_bytes=64)

        def mx_pair(name, cols):
            return sbuf(name + "_codes", [P, cols], U32), sbuf(name + "_scales", [P, cols], U8)

        score = [[ps.tile([P, BANK], F32, name="score%d%d" % (g, b)) for b in range(2)] for g in range(2)]
        ybank = [ps.tile([P, BANK], F32, name="y%d" % b) for b in range(4)]

        nu = len(UNITS)
        width = [u[2] for u in UNITS]
        first = [sum(2 * w // P for w in width[:u]) for u in range(nu)]

        k_raw = sbuf("k_raw", [P, PACK, N], F32)
        k_bf = sbuf("k_bf", [P, N * PACK], BF16)
        k_mx = mx_pair("k", N)
        v_raw = sbuf("v_raw", [P, KV, PACK, E], F32)
        v_bf = sbuf("v_bf", [P, KV * E * PACK], BF16)
        v_mx = mx_pair("v", KV * E)
        t_sb = sbuf("t_sb", [P, PACK], F32)
        t_run = sbuf("t_run", [P, PACK, WRUN], F32)
        kb_sb = sbuf("kb_sb", [P, PACK], F32)
        gn_sb = sbuf("gn_sb", [P, E], F32)
        q_raw = [sbuf("q_raw%d" % u, [P, PACK, width[u]], F32) for u in range(nu)]
        q_bf = [sbuf("q_bf%d" % u, [P, width[u] * PACK], BF16) for u in range(nu)]
        q_mx = [mx_pair("q%d" % u, width[u]) for u in range(nu)]
        p_sb = [[sbuf("p%d%d" % (u, g), [P, PACK, width[u]], F32) for g in range(2)] for u in range(nu)]
        w_bf = [[sbuf("w%d%d" % (u, g), [P, width[u] * PACK], BF16) for g in range(2)] for u in range(nu)]
        w_mx = [[mx_pair("w%d%d" % (u, g), width[u]) for g in range(2)] for u in range(nu)]
        o_sb = [[sbuf("o%d%d" % (u, g), [P, width[u]], F32) for g in range(2)] for u in range(nu)]
        squares = sbuf("squares", [P, 16 * E], BF16)
        ssq = sbuf("ssq", [P, 16], F32)
        rstd = sbuf("rstd", [P, 16], F32)
        warm = sbuf("warm", [P, 8], F32)

        q_rows = qT.rearrange("h d n -> (h d) n")
        k_rows = kT.rearrange("h (p j) n -> (h p) j n", j=PACK)

        def copy(engine, dst, src):
            if engine == "act":
                nc.scalar.copy(out=dst, in_=src)
            else:
                nc.vector.tensor_copy(out=dst, in_=src)

        def load_q(u, g=None):
            pair, q0, w = UNITS[u]
            queue = nc.scalar if g == 1 else nc.sync
            if g is None:
                rows = q_rows[PAIRS[pair][0] * D : (PAIRS[pair][1] + 1) * D, q0 : q0 + w]
                queue.dma_start(out=q_raw[u][:], in_=rows.rearrange("(p j) n -> p j n", j=PACK))
            else:
                rows = q_rows[PAIRS[pair][g] * D : (PAIRS[pair][g] + 1) * D, q0 : q0 + w]
                queue.dma_start(out=q_raw[u][g * ROWS : (g + 1) * ROWS], in_=rows.rearrange("(p j) n -> p j n", j=PACK))

        def load_k(lo, hi):
            nc.sync.dma_start(out=k_raw[:, :, lo:hi], in_=k_rows[:, :, lo:hi])

        def spread_k(engine, lo, hi):
            dst = k_bf[:].rearrange("p (r s j) -> p s j r", r=PACK, j=PACK)[:, lo:hi]
            src = k_raw[:].rearrange("p j (s r) -> p s j r", r=PACK)[:, lo:hi]
            copy(engine, dst, src)

        def spread_q(u, engine, lo, hi):
            n = width[u] // P
            run = RUN if engine == "dve" or n == 1 else n
            dst = q_bf[u][:].rearrange("p (i c m j) -> p c j m i", i=n, m=run // n, j=PACK)[:, lo // run : hi // run]
            src = q_raw[u][:].rearrange("p j (c m i) -> p c j m i", i=n, m=run // n)[:, lo // run : hi // run]
            copy(engine, dst, src)

        def spread_v(kv, engine):
            dst = v_bf[:, kv * E * PACK : (kv + 1) * E * PACK].rearrange("p (c i j) -> p c j i", i=RUN, j=PACK)
            src = v_raw[:, kv].rearrange("p j (c i) -> p c j i", i=RUN)
            copy(engine, dst, src)

        def quantize(mx, bf, lo, hi):
            nc.vector.quantize_mx(out=mx[0][:, lo:hi].bitcast(FP8X4), scales=mx[1][:, lo:hi], in_=bf[:, lo * PACK : hi * PACK])

        def matmul(dst, a, a_at, b, b_at, rows):
            nc.tensor.matmul_mx(
                out=dst,
                lhsT=a[0][rows, a_at : a_at + P].bitcast(FP8X4),
                lhsT_scale=a[1][rows, a_at : a_at + P],
                rhs=b[0][rows, b_at : b_at + P].bitcast(FP8X4),
                rhs_scale=b[1][rows, b_at : b_at + P],
                start=True,
                stop=True,
            )

        def place(u, g, r):
            per_bank = BANK // width[u]
            base = sum(PACK * w // BANK for w in width[:u])
            return score[g][(base + r // per_bank) % 2], (r % per_bank) * width[u]

        def scores(u, rs):
            for r in rs:
                for c in range(0, width[u], P):
                    for g in range(2):
                        bank, at = place(u, g, r)
                        matmul(bank[:, at + c : at + c + P], k_mx, r * P, q_mx[u], c, slice(g * ROWS, (g + 1) * ROWS))

        def tanh(u, g, rs):
            for r in rs:
                bank, at = place(u, g, r)
                nc.scalar.activation(
                    out=p_sb[u][g][:, r, :],
                    in_=bank[:, at : at + width[u]],
                    func=ACT.Tanh,
                    bias=kb_sb[:, r : r + 1],
                )

        def weigh(u, g):
            nc.vector.tensor_tensor(
                out=w_bf[u][g][:].rearrange("p (c i r) -> p c r i", i=WRUN, r=PACK),
                in0=p_sb[u][g][:].rearrange("p r (c i) -> p c r i", i=WRUN),
                in1=t_run[:].unsqueeze(1).to_broadcast([P, width[u] // WRUN, PACK, WRUN]),
                op=ALU.mult,
            )

        def quant_w(u, g):
            quantize(w_mx[u][g], w_bf[u][g], 0, width[u])

        def tiles(u, g):
            n = width[u] // P
            return range(first[u] + g * n, first[u] + (g + 1) * n)

        def y_of(i):
            return ybank[i // 4][:, (i % 4) * E : (i % 4 + 1) * E]

        def values(u, g):
            for n, i in enumerate(tiles(u, g)):
                matmul(y_of(i), w_mx[u][g], n * P, v_mx, g * E, slice(0, P))

        def sum_squares(u, g):
            for i in tiles(u, g):
                nc.scalar.activation(out=squares[:, i * E : (i + 1) * E], in_=y_of(i), func=ACT.Square, accum_out=ssq[:, i : i + 1])

        def roots(lo, hi):
            nc.scalar.activation(out=rstd[:, lo:hi], in_=ssq[:, lo:hi], func=ACT.Abs_reciprocal_sqrt, scale=1.0 / E, bias=256 * 1e-5)

        def finish(u, g):
            pair, q0, w = UNITS[u]
            for n, i in enumerate(tiles(u, g)):
                nc.vector.scalar_tensor_tensor(
                    out=o_sb[u][g][:, n * E : (n + 1) * E], in0=y_of(i), scalar=rstd[:, i : i + 1], in1=gn_sb[:], op0=ALU.mult, op1=ALU.mult
                )
            rows = out[PAIRS[pair][g], q0 : q0 + w, :].rearrange("(m i) e -> m (i e)", m=P)
            nc.sync.dma_start(out=rows, in_=o_sb[u][g][:])

        def load_small():
            nc.scalar.dma_start(out=kb_sb[:], in_=kb.rearrange("(p j) o -> p (j o)", j=PACK))
            nc.scalar.dma_start(out=t_sb[:], in_=t.rearrange("(p j) o -> p (j o)", j=PACK))
            nc.vector.memset(warm[:, 0:1], 1.0)
            nc.scalar.activation(out=warm[:, 1:2], in_=warm[:, 0:1], func=ACT.Tanh)

        def spread_t():
            nc.vector.tensor_copy(out=t_run[:], in_=t_sb[:].unsqueeze(2).to_broadcast([P, PACK, WRUN]))

        def load_v():
            nc.sync.dma_start(out=v_raw[:], in_=v.rearrange("h (p j) e -> p h j e", j=PACK))

        def load_gn():
            nc.sync.dma_start(out=gn_sb[:], in_=gn)

        def quant_k(lo, hi):
            quantize(k_mx, k_bf, lo * P, hi * P)

        def quant_q(u):
            quantize(q_mx[u], q_bf[u], 0, width[u])

        def quant_v():
            quantize(v_mx, v_bf, 0, KV * E)

        steps = {
            "load_small": load_small, "load_k": load_k, "load_q": load_q, "load_v": load_v, "load_gn": load_gn, "spread_t": spread_t,
            "spread_k": spread_k, "spread_q": spread_q, "spread_v": spread_v,
            "quant_k": quant_k, "quant_q": quant_q, "quant_v": quant_v, "quant_w": quant_w,
            "scores": scores, "tanh": tanh, "weigh": weigh, "values": values,
            "sum_squares": sum_squares, "roots": roots, "finish": finish,
        }
        for step in ORDER:
            steps[step[0]](*step[1:])
